import numpy as np, ml_dtypes
CORES = [16,23,24,31,64,71]
N = 6
TK = 256
COEF = [[-2,3,-1,-1,1,-1],[-2,3,3,1,-1,-1],[-2,1,-1,-2,-1,-1],[1,3,3,-1,2,2],[-2,3,2,1,3,2],[1,2,-1,-1,2,2]]
def setup_inputs(rng):
    return {"x": rng.standard_normal((N, 128, TK), dtype=np.float32).astype(ml_dtypes.bfloat16), "a": (rng.standard_normal((N, 128, 128), dtype=np.float32) / 11).astype(ml_dtypes.bfloat16)}
def setup_inputs_big(rng):
    d = setup_inputs(rng)
    for k in ("x", "a"): d[k] = (d[k].astype(np.float32) * 1024.0).astype(d[k].dtype)
    return d
def setup_inputs_small(rng):
    d = setup_inputs(rng)
    for k in ("x", "a"): d[k] = (d[k].astype(np.float32) * (1 / 1024.0)).astype(d[k].dtype)
    return d
def setup_inputs_apart(rng):
    d = setup_inputs(rng)
    f = (10.0 ** rng.permutation(np.linspace(-1.5, 1.5, N))).astype(np.float32).reshape(N, 1, 1)
    for k in ("x", "a"): d[k] = (d[k].astype(np.float32) * f).astype(d[k].dtype)
    return d
def reference(x, a):
    X, A = x.astype(np.float64), a.astype(np.float64)
    y = np.stack([A[r].T @ sum(COEF[r][j] * X[j] for j in range(N)) for r in range(N)])
    return {"y": y.astype(ml_dtypes.bfloat16)}

@@ -1,0 +1,204 @@
+from concourse.bass import DstId, RemoteDMATransfer
+from concourse.mybir import AluOpType
+
+P, W, M = 128, 256, 128
+NSEND = 7
+NE = 8
+MAX_GATE = 3
+BF, F32 = "bfloat16", "float32"
+
+SCRATCH = {
+    "xo": ("sbuf", [P, W], BF), "asb": ("sbuf", [P, M], BF), "ysb": ("sbuf", [P, W], BF),
+    "xd": ("dram", [P, W], BF), "rl": ("dram", [P, W], BF),
+    "acc": ("psum", [P, 512], F32),
+}
+for _k in range(NSEND):
+    SCRATCH["b%d" % _k] = ("sbuf", [P, W], BF)
+for _k in range(3):
+    SCRATCH["kx%d" % _k] = ("sbuf", [P, W], BF)
+    SCRATCH["pg%d" % _k] = ("psum", [P, 512], F32)
+    SCRATCH["cb%d" % _k] = ("sbuf", [P, W], BF)
+for _k in range(4):
+    SCRATCH["ka%d" % _k] = ("sbuf", [P, M], BF)
+    SCRATCH["as%d" % _k] = ("sbuf", [P, M], BF)
+
+SEMAPHORES = (["sx", "sxd", "sa", "sy", "ls", "vk", "vg", "va", "vy", "pm", "vc0", "vc1", "vc2"]
+              + ["m%d" % _k for _k in range(NSEND)])
+
+
+def make_plan(cores, C, topo):
+    n = len(cores)
+    on = {}
+    for r in range(n):
+        on.setdefault(topo.chip(cores[r]), []).append(r)
+    raw = {r: [] for r in range(n)}
+    groups = {r: [] for r in range(n)}
+    terms = {r: [] for r in range(n)}
+    relays = []
+    for ch in sorted(on):
+        p, q = on[ch]
+        peer = {p: q, q: p}
+        for s in (p, q):
+            raw[s].append(peer[s])
+            terms[s].append((0, None, C[s][s]))
+            terms[s].append((1, peer[s], C[s][peer[s]]))
+        far = [r for r in range(n) if r not in (p, q)]
+        can = {r: [s for s in (p, q) if topo.may_write(cores[s], cores[r])] for r in far}
+        load = {p: [], q: []}
+        for r in sorted(far, key=lambda r: len(can[r])):
+            s = min(can[r], key=lambda s: len(load[s]))
+            load[s].append(r)
+        for s in (p, q):
+            z = peer[s]
+            gam = {r: C[r][s] / C[r][z] for r in load[s]}
+            if len(load[s]) > MAX_GATE and not relays:
+                near = [r for r in load[s] if topo.mates(ch, topo.chip(cores[r]))] or load[s]
+                d = min(near, key=lambda d: len(set(gam[r] for r in load[s] if r != d)))
+                hs = [h for h in range(topo.CHIPS * topo.CORES_PER_CHIP)
+                      if topo.chip(h) == ch and h not in cores and topo.may_write(h, cores[d])]
+                h = min(hs, key=lambda h: (topo.die(h) == topo.die(cores[s]), h))
+                relays.append((z, h, d))
+                load[s].remove(d)
+                raw[s].append(d)
+                terms[d].append((2, s, C[d][s]))
+                terms[d].append((9, n, C[d][z]))
+            gs = []
+            for r in load[s]:
+                hit = [g for g in gs if g[0] == gam[r]]
+                if hit:
+                    hit[0][1].append(r)
+                else:
+                    gs.append([gam[r], [r]])
+            gs.sort(key=lambda g: -len(g[1]))
+            groups[s] = gs
+            for i in range(len(gs)):
+                for r in gs[i][1]:
+                    terms[r].append((3 + i, s, C[r][z]))
+    for r in range(n):
+        terms[r].sort(key=lambda t: t[0])
+    return raw, groups, terms, relays
+
+
+def engines(topo, core, dsts):
+    m = topo.mask(core, dsts[0])
+    for d in dsts[1:]:
+        m &= topo.mask(core, d)
+    out, k, bit = 0, 0, 1
+    while k < NE:
+        if m & bit:
+            out |= bit
+            k += 1
+        bit <<= 1
+    return out
+
+
+def rank_program(g, core, T, topo):
+    cores = list(T.cores)
+    n = len(cores)
+    C = T.tables["COEF"]
+    raw, groups, terms, relays = make_plan(cores, C, topo)
+    S = T.sem
+
+    def send(src, name, sem, dsts, mask):
+        ids = [DstId(rid=topo.addr(d)[0], pnc=topo.addr(d)[1]) for d in dsts]
+        g.remote_dma_fused([RemoteDMATransfer(dst_ids=ids, dma_engine_mask=mask, remote_sem=sem, srcs=[src],
+                                              dsts=[T[name][:] for _ in dsts], alu_op=0)], local_sem=S.ls)
+
+    for z, h, d in relays:
+        if core == h:
+            g.wait_ge(S["m%d" % z], NE)
+            send(T.rl[:], "b%d" % n, S["m%d" % n], [cores[d]], engines(topo, core, [cores[d]]))
+            g.wait_ge(S.ls, NE)
+    r = T.rank_of(core)
+    if r is None:
+        return
+    my_relays = [t for t in relays if t[0] == r]
+    gs = groups[r]
+    peer = raw[r][0]
+    everyone = [cores[d] for d in raw[r]] + [t[1] for t in my_relays] + [cores[d] for gq in gs for d in gq[1]]
+    mask = engines(topo, core, everyone)
+
+    g.sync.dma_start(T.xo[:], T.x[:]).then_inc(S.sx, 16)
+    if my_relays:
+        g.sync.dma_start(T.xd[:], T.x[:]).then_inc(S.sxd, 16)
+    g.sync.dma_start(T.asb[:], T.a[:]).then_inc(S.sa, 16)
+
+    calls = 0
+    g.wait_ge(S.sx, 16)
+    send(T.xo[:], "b%d" % r, S["m%d" % r], [cores[d] for d in raw[r]], mask)
+    calls += 1
+    for z, h, d in my_relays:
+        g.wait_ge(S.sxd, 16)
+        send(T.xd[:], "rl", S["m%d" % r], [h], mask)
+        calls += 1
+    for i in range(len(gs)):
+        g.wait_ge(S["vc%d" % i], 1)
+        send(T["cb%d" % i][:], "b%d" % r, S["m%d" % r], [cores[d] for d in gs[i][1]], mask)
+        calls += 1
+    g.wait_ge(S.ls, NE * calls)
+
+    v = g.vector
+    mags = []
+    for gq in gs:
+        if abs(gq[0]) == 1:
+            if 1 not in mags:
+                mags.append(1)
+        elif gq[0] not in mags:
+            mags.append(gq[0])
+    mults = []
+    for t in terms[r]:
+        if t[2] != 1 and t[2] not in mults:
+            mults.append(t[2])
+    nk = 0
+    for k in range(len(mags)):
+        if mags[k] != 1:
+            v.memset(T["kx%d" % k][:], float(mags[k])).then_inc(S.vk, 1)
+            nk += 1
+    for k in range(len(mults)):
+        v.memset(T["ka%d" % k][:], float(mults[k])).then_inc(S.vk, 1)
+        nk += 1
+    if nk:
+        v.wait_ge(S.vk, nk)
+    if gs:
+        v.wait_ge(S.sx, 16)
+        for k in range(len(mags)):
+            pg = T["pg%d" % k][:, 0:W]
+            if mags[k] == 1:
+                v.tensor_copy(pg, T.xo[:]).then_inc(S.vg, 1)
+            else:
+                v.tensor_tensor(pg, T.xo[:], T["kx%d" % k][:], AluOpType.mult).then_inc(S.vg, 1)
+        v.wait_ge(S.vg, len(mags))
+        v.wait_ge(S["m%d" % peer], NE)
+        for i in range(len(gs)):
+            gm = gs[i][0]
+            k = mags.index(1 if abs(gm) == 1 else gm)
+            op = AluOpType.subtract if gm == -1 else AluOpType.add
+            v.tensor_tensor(T["cb%d" % i][:], T["b%d" % peer][:], T["pg%d" % k][:, 0:W], op).then_inc(S["vc%d" % i], 1)
+    if mults:
+        v.wait_ge(S.sa, 16)
+        for k in range(len(mults)):
+            v.tensor_tensor(T["as%d" % k][:], T.asb[:], T["ka%d" % k][:], AluOpType.mult).then_inc(S.va, 1)
+    v.wait_ge(S.pm, 1)
+    v.tensor_copy(T.ysb[:], T.acc[:, 0:W]).then_inc(S.vy, 1)
+
+    te = g.tensor
+    te.wait_ge(S.sa, 16)
+    if mults:
+        te.wait_ge(S.va, len(mults))
+    last = len(terms[r]) - 1
+    for i in range(last + 1):
+        _, s, m = terms[r][i]
+        if s is None:
+            te.wait_ge(S.sx, 16)
+            rhs = T.xo[:]
+        else:
+            te.wait_ge(S["m%d" % s], NE)
+            rhs = T["b%d" % s][:]
+        lhs = T.asb[:] if m == 1 else T["as%d" % mults.index(m)][:]
+        mm = te.matmul(T.acc[:, 0:W], lhs, rhs, i == 0, i == last)
+        if i == last:
+            mm.then_inc(S.pm, 1)
+
+    g.sync.wait_ge(S.vy, 1)
+    g.sync.dma_start(T.y[:], T.ysb[:]).then_inc(S.sy, 16)
+    g.sync.wait_ge(S.sy, 16)

@@ -2,9 +2,9 @@ from concourse.bass import DstId, RemoteDMATransfer
 from concourse.mybir import AluOpType
 
 P, W, M = 128, 256, 128
-NSEND = 7
+NR = 6
 NE = 8
-MAX_GATE = 3
+MAX_GATE = 2
 BF, F32 = "bfloat16", "float32"
 
 SCRATCH = {
@@ -12,18 +12,18 @@ SCRATCH = {
     "xd": ("dram", [P, W], BF), "rl": ("dram", [P, W], BF),
     "acc": ("psum", [P, 512], F32),
 }
-for _k in range(NSEND):
+for _k in range(NR):
     SCRATCH["b%d" % _k] = ("sbuf", [P, W], BF)
 for _k in range(3):
     SCRATCH["kx%d" % _k] = ("sbuf", [P, W], BF)
     SCRATCH["pg%d" % _k] = ("psum", [P, 512], F32)
     SCRATCH["cb%d" % _k] = ("sbuf", [P, W], BF)
-for _k in range(4):
+for _k in range(5):
     SCRATCH["ka%d" % _k] = ("sbuf", [P, M], BF)
     SCRATCH["as%d" % _k] = ("sbuf", [P, M], BF)
 
 SEMAPHORES = (["sx", "sxd", "sa", "sy", "ls", "vk", "vg", "va", "vy", "pm", "vc0", "vc1", "vc2"]
-              + ["m%d" % _k for _k in range(NSEND)])
+              + ["m%d" % _k for _k in range(NR)])
 
 
 def make_plan(cores, C, topo):
@@ -31,15 +31,16 @@ def make_plan(cores, C, topo):
     on = {}
     for r in range(n):
         on.setdefault(topo.chip(cores[r]), []).append(r)
+    peer = {}
     raw = {r: [] for r in range(n)}
+    fwd = {r: [] for r in range(n)}
     groups = {r: [] for r in range(n)}
     terms = {r: [] for r in range(n)}
     relays = []
     for ch in sorted(on):
         p, q = on[ch]
-        peer = {p: q, q: p}
+        peer[p], peer[q] = q, p
         for s in (p, q):
-            raw[s].append(peer[s])
             terms[s].append((0, None, C[s][s]))
             terms[s].append((1, peer[s], C[s][peer[s]]))
         far = [r for r in range(n) if r not in (p, q)]
@@ -51,17 +52,29 @@ def make_plan(cores, C, topo):
         for s in (p, q):
             z = peer[s]
             gam = {r: C[r][s] / C[r][z] for r in load[s]}
-            if len(load[s]) > MAX_GATE and not relays:
-                near = [r for r in load[s] if topo.mates(ch, topo.chip(cores[r]))] or load[s]
+            first = []
+            if load[s]:
+                far2 = [r for r in load[s] if not topo.mates(ch, topo.chip(cores[r]))] or load[s]
+                first = [min(far2, key=lambda d: abs(gam[d]) == 1)]
+            while len(load[s]) > MAX_GATE:
+                near = [r for r in load[s] if topo.mates(ch, topo.chip(cores[r])) and r not in first]
+                near = near or [r for r in load[s] if r not in first]
                 d = min(near, key=lambda d: len(set(gam[r] for r in load[s] if r != d)))
                 hs = [h for h in range(topo.CHIPS * topo.CORES_PER_CHIP)
-                      if topo.chip(h) == ch and h not in cores and topo.may_write(h, cores[d])]
+                      if topo.chip(h) == ch and h not in cores and topo.may_write(h, cores[d])
+                      and h not in [t[1] for t in relays]]
                 h = min(hs, key=lambda h: (topo.die(h) == topo.die(cores[s]), h))
                 relays.append((z, h, d))
                 load[s].remove(d)
                 raw[s].append(d)
                 terms[d].append((2, s, C[d][s]))
-                terms[d].append((9, n, C[d][z]))
+                terms[d].append((9, z, C[d][z]))
+            for d in first:
+                load[s].remove(d)
+                raw[s].insert(0, d)
+                fwd[s].append(d)
+                terms[d].append((2, s, C[d][s]))
+                terms[d].append((3, z, C[d][z]))
             gs = []
             for r in load[s]:
                 hit = [g for g in gs if g[0] == gam[r]]
@@ -73,18 +86,21 @@ def make_plan(cores, C, topo):
             groups[s] = gs
             for i in range(len(gs)):
                 for r in gs[i][1]:
-                    terms[r].append((3 + i, s, C[r][z]))
+                    terms[r].append((4 + i, s, C[r][z]))
     for r in range(n):
         terms[r].sort(key=lambda t: t[0])
-    return raw, groups, terms, relays
+    return peer, raw, fwd, groups, terms, relays
 
 
-def engines(topo, core, dsts):
+def engines(topo, core, dsts, skip=0):
     m = topo.mask(core, dsts[0])
     for d in dsts[1:]:
         m &= topo.mask(core, d)
+    m &= ~skip
     out, k, bit = 0, 0, 1
     while k < NE:
+        if bit > m:
+            return 0
         if m & bit:
             out |= bit
             k += 1
@@ -94,9 +110,8 @@ def engines(topo, core, dsts):
 
 def rank_program(g, core, T, topo):
     cores = list(T.cores)
-    n = len(cores)
     C = T.tables["COEF"]
-    raw, groups, terms, relays = make_plan(cores, C, topo)
+    peers, raw, fwd, groups, terms, relays = make_plan(cores, C, topo)
     S = T.sem
 
     def send(src, name, sem, dsts, mask):
@@ -107,33 +122,45 @@ def rank_program(g, core, T, topo):
     for z, h, d in relays:
         if core == h:
             g.wait_ge(S["m%d" % z], NE)
-            send(T.rl[:], "b%d" % n, S["m%d" % n], [cores[d]], engines(topo, core, [cores[d]]))
+            send(T.rl[:], "b%d" % z, S["m%d" % z], [cores[d]], engines(topo, core, [cores[d]]))
             g.wait_ge(S.ls, NE)
     r = T.rank_of(core)
     if r is None:
         return
-    my_relays = [t for t in relays if t[0] == r]
+    helpers = [t[1] for t in relays if t[0] == r]
     gs = groups[r]
-    peer = raw[r][0]
-    everyone = [cores[d] for d in raw[r]] + [t[1] for t in my_relays] + [cores[d] for gq in gs for d in gq[1]]
+    peer = peers[r]
+    mine, theirs = "b%d" % r, "b%d" % peer
+    sm, st = S["m%d" % r], S["m%d" % peer]
+    everyone = [cores[peer]] + [cores[d] for d in raw[r]] + helpers + [cores[d] for gq in gs for d in gq[1]]
     mask = engines(topo, core, everyone)
+    side = 0 if (fwd[peer] or groups[peer] or not raw[r]) else engines(topo, core, [cores[peer]], mask)
 
     g.sync.dma_start(T.xo[:], T.x[:]).then_inc(S.sx, 16)
-    if my_relays:
+    if helpers:
         g.sync.dma_start(T.xd[:], T.x[:]).then_inc(S.sxd, 16)
     g.sync.dma_start(T.asb[:], T.a[:]).then_inc(S.sa, 16)
 
-    calls = 0
+    calls = 1
     g.wait_ge(S.sx, 16)
-    send(T.xo[:], "b%d" % r, S["m%d" % r], [cores[d] for d in raw[r]], mask)
-    calls += 1
-    for z, h, d in my_relays:
+    if not side:
+        send(T.xo[:], mine, sm, [cores[peer]], mask)
+    if helpers:
         g.wait_ge(S.sxd, 16)
-        send(T.xd[:], "rl", S["m%d" % r], [h], mask)
+        send(T.xd[:], "rl", sm, helpers, mask)
+        calls += 1
+    if raw[r]:
+        send(T.xo[:], mine, sm, [cores[d] for d in raw[r]], mask)
+        calls += 1
+    if side:
+        send(T.xo[:], mine, sm, [cores[peer]], side)
+    if fwd[r]:
+        g.wait_ge(st, NE)
+        send(T[theirs][:], theirs, st, [cores[d] for d in fwd[r]], mask)
         calls += 1
     for i in range(len(gs)):
         g.wait_ge(S["vc%d" % i], 1)
-        send(T["cb%d" % i][:], "b%d" % r, S["m%d" % r], [cores[d] for d in gs[i][1]], mask)
+        send(T["cb%d" % i][:], mine, sm, [cores[d] for d in gs[i][1]], mask)
         calls += 1
     g.wait_ge(S.ls, NE * calls)
 
@@ -168,12 +195,12 @@ def rank_program(g, core, T, topo):
             else:
                 v.tensor_tensor(pg, T.xo[:], T["kx%d" % k][:], AluOpType.mult).then_inc(S.vg, 1)
         v.wait_ge(S.vg, len(mags))
-        v.wait_ge(S["m%d" % peer], NE)
+        v.wait_ge(st, NE)
         for i in range(len(gs)):
             gm = gs[i][0]
             k = mags.index(1 if abs(gm) == 1 else gm)
             op = AluOpType.subtract if gm == -1 else AluOpType.add
-            v.tensor_tensor(T["cb%d" % i][:], T["b%d" % peer][:], T["pg%d" % k][:, 0:W], op).then_inc(S["vc%d" % i], 1)
+            v.tensor_tensor(T["cb%d" % i][:], T[theirs][:], T["pg%d" % k][:, 0:W], op).then_inc(S["vc%d" % i], 1)
     if mults:
         v.wait_ge(S.sa, 16)
         for k in range(len(mults)):

from concourse.bass import DstId, RemoteDMATransfer
from concourse.mybir import AluOpType

P, W, M = 128, 256, 128
NR = 6
NE = 8
MAX_GATE = 2
BF, F32 = "bfloat16", "float32"

SCRATCH = {
    "xo": ("sbuf", [P, W], BF), "asb": ("sbuf", [P, M], BF), "ysb": ("sbuf", [P, W], BF),
    "xd": ("dram", [P, W], BF), "rl": ("dram", [P, W], BF),
    "acc": ("psum", [P, 512], F32),
}
for _k in range(NR):
    SCRATCH["b%d" % _k] = ("sbuf", [P, W], BF)
for _k in range(3):
    SCRATCH["kx%d" % _k] = ("sbuf", [P, W], BF)
    SCRATCH["pg%d" % _k] = ("psum", [P, 512], F32)
    SCRATCH["cb%d" % _k] = ("sbuf", [P, W], BF)
for _k in range(5):
    SCRATCH["ka%d" % _k] = ("sbuf", [P, M], BF)
    SCRATCH["as%d" % _k] = ("sbuf", [P, M], BF)

SEMAPHORES = (["sx", "sxd", "sa", "sy", "ls", "vk", "vg", "va", "vy", "pm", "vc0", "vc1", "vc2"]
              + ["m%d" % _k for _k in range(NR)])


def make_plan(cores, C, topo):
    n = len(cores)
    on = {}
    for r in range(n):
        on.setdefault(topo.chip(cores[r]), []).append(r)
    peer = {}
    raw = {r: [] for r in range(n)}
    fwd = {r: [] for r in range(n)}
    groups = {r: [] for r in range(n)}
    terms = {r: [] for r in range(n)}
    relays = []
    for ch in sorted(on):
        p, q = on[ch]
        peer[p], peer[q] = q, p
        for s in (p, q):
            terms[s].append((0, None, C[s][s]))
            terms[s].append((1, peer[s], C[s][peer[s]]))
        far = [r for r in range(n) if r not in (p, q)]
        can = {r: [s for s in (p, q) if topo.may_write(cores[s], cores[r])] for r in far}
        load = {p: [], q: []}
        for r in sorted(far, key=lambda r: len(can[r])):
            s = min(can[r], key=lambda s: len(load[s]))
            load[s].append(r)
        for s in (p, q):
            z = peer[s]
            gam = {r: C[r][s] / C[r][z] for r in load[s]}
            first = []
            if load[s]:
                far2 = [r for r in load[s] if not topo.mates(ch, topo.chip(cores[r]))] or load[s]
                first = [min(far2, key=lambda d: abs(gam[d]) == 1)]
            while len(load[s]) > MAX_GATE:
                near = [r for r in load[s] if topo.mates(ch, topo.chip(cores[r])) and r not in first]
                near = near or [r for r in load[s] if r not in first]
                d = min(near, key=lambda d: len(set(gam[r] for r in load[s] if r != d)))
                hs = [h for h in range(topo.CHIPS * topo.CORES_PER_CHIP)
                      if topo.chip(h) == ch and h not in cores and topo.may_write(h, cores[d])
                      and h not in [t[1] for t in relays]]
                h = min(hs, key=lambda h: (topo.die(h) == topo.die(cores[s]), h))
                relays.append((z, h, d))
                load[s].remove(d)
                raw[s].append(d)
                terms[d].append((2, s, C[d][s]))
                terms[d].append((9, z, C[d][z]))
            for d in first:
                load[s].remove(d)
                raw[s].insert(0, d)
                fwd[s].append(d)
                terms[d].append((2, s, C[d][s]))
                terms[d].append((3, z, C[d][z]))
            gs = []
            for r in load[s]:
                hit = [g for g in gs if g[0] == gam[r]]
                if hit:
                    hit[0][1].append(r)
                else:
                    gs.append([gam[r], [r]])
            gs.sort(key=lambda g: -len(g[1]))
            groups[s] = gs
            for i in range(len(gs)):
                for r in gs[i][1]:
                    terms[r].append((4 + i, s, C[r][z]))
    for r in range(n):
        terms[r].sort(key=lambda t: t[0])
    return peer, raw, fwd, groups, terms, relays


def engines(topo, core, dsts, skip=0):
    m = topo.mask(core, dsts[0])
    for d in dsts[1:]:
        m &= topo.mask(core, d)
    m &= ~skip
    out, k, bit = 0, 0, 1
    while k < NE:
        if bit > m:
            return 0
        if m & bit:
            out |= bit
            k += 1
        bit <<= 1
    return out


def rank_program(g, core, T, topo):
    cores = list(T.cores)
    C = T.tables["COEF"]
    peers, raw, fwd, groups, terms, relays = make_plan(cores, C, topo)
    S = T.sem

    def send(src, name, sem, dsts, mask):
        ids = [DstId(rid=topo.addr(d)[0], pnc=topo.addr(d)[1]) for d in dsts]
        g.remote_dma_fused([RemoteDMATransfer(dst_ids=ids, dma_engine_mask=mask, remote_sem=sem, srcs=[src],
                                              dsts=[T[name][:] for _ in dsts], alu_op=0)], local_sem=S.ls)

    for z, h, d in relays:
        if core == h:
            g.wait_ge(S["m%d" % z], NE)
            send(T.rl[:], "b%d" % z, S["m%d" % z], [cores[d]], engines(topo, core, [cores[d]]))
            g.wait_ge(S.ls, NE)
    r = T.rank_of(core)
    if r is None:
        return
    helpers = [t[1] for t in relays if t[0] == r]
    gs = groups[r]
    peer = peers[r]
    mine, theirs = "b%d" % r, "b%d" % peer
    sm, st = S["m%d" % r], S["m%d" % peer]
    everyone = [cores[peer]] + [cores[d] for d in raw[r]] + helpers + [cores[d] for gq in gs for d in gq[1]]
    mask = engines(topo, core, everyone)
    side = 0 if (fwd[peer] or groups[peer] or not raw[r]) else engines(topo, core, [cores[peer]], mask)

    g.sync.dma_start(T.xo[:], T.x[:]).then_inc(S.sx, 16)
    if helpers:
        g.sync.dma_start(T.xd[:], T.x[:]).then_inc(S.sxd, 16)
    g.sync.dma_start(T.asb[:], T.a[:]).then_inc(S.sa, 16)

    calls = 1
    g.wait_ge(S.sx, 16)
    if not side:
        send(T.xo[:], mine, sm, [cores[peer]], mask)
    if helpers:
        g.wait_ge(S.sxd, 16)
        send(T.xd[:], "rl", sm, helpers, mask)
        calls += 1
    if raw[r]:
        send(T.xo[:], mine, sm, [cores[d] for d in raw[r]], mask)
        calls += 1
    if side:
        send(T.xo[:], mine, sm, [cores[peer]], side)
    if fwd[r]:
        g.wait_ge(st, NE)
        send(T[theirs][:], theirs, st, [cores[d] for d in fwd[r]], mask)
        calls += 1
    for i in range(len(gs)):
        g.wait_ge(S["vc%d" % i], 1)
        send(T["cb%d" % i][:], mine, sm, [cores[d] for d in gs[i][1]], mask)
        calls += 1
    g.wait_ge(S.ls, NE * calls)

    v = g.vector
    mags = []
    for gq in gs:
        if abs(gq[0]) == 1:
            if 1 not in mags:
                mags.append(1)
        elif gq[0] not in mags:
            mags.append(gq[0])
    mults = []
    for t in terms[r]:
        if t[2] != 1 and t[2] not in mults:
            mults.append(t[2])
    nk = 0
    for k in range(len(mags)):
        if mags[k] != 1:
            v.memset(T["kx%d" % k][:], float(mags[k])).then_inc(S.vk, 1)
            nk += 1
    for k in range(len(mults)):
        v.memset(T["ka%d" % k][:], float(mults[k])).then_inc(S.vk, 1)
        nk += 1
    if nk:
        v.wait_ge(S.vk, nk)
    if gs:
        v.wait_ge(S.sx, 16)
        for k in range(len(mags)):
            pg = T["pg%d" % k][:, 0:W]
            if mags[k] == 1:
                v.tensor_copy(pg, T.xo[:]).then_inc(S.vg, 1)
            else:
                v.tensor_tensor(pg, T.xo[:], T["kx%d" % k][:], AluOpType.mult).then_inc(S.vg, 1)
        v.wait_ge(S.vg, len(mags))
        v.wait_ge(st, NE)
        for i in range(len(gs)):
            gm = gs[i][0]
            k = mags.index(1 if abs(gm) == 1 else gm)
            op = AluOpType.subtract if gm == -1 else AluOpType.add
            v.tensor_tensor(T["cb%d" % i][:], T[theirs][:], T["pg%d" % k][:, 0:W], op).then_inc(S["vc%d" % i], 1)
    if mults:
        v.wait_ge(S.sa, 16)
        for k in range(len(mults)):
            v.tensor_tensor(T["as%d" % k][:], T.asb[:], T["ka%d" % k][:], AluOpType.mult).then_inc(S.va, 1)
    v.wait_ge(S.pm, 1)
    v.tensor_copy(T.ysb[:], T.acc[:, 0:W]).then_inc(S.vy, 1)

    te = g.tensor
    te.wait_ge(S.sa, 16)
    if mults:
        te.wait_ge(S.va, len(mults))
    last = len(terms[r]) - 1
    for i in range(last + 1):
        _, s, m = terms[r][i]
        if s is None:
            te.wait_ge(S.sx, 16)
            rhs = T.xo[:]
        else:
            te.wait_ge(S["m%d" % s], NE)
            rhs = T["b%d" % s][:]
        lhs = T.asb[:] if m == 1 else T["as%d" % mults.index(m)][:]
        mm = te.matmul(T.acc[:, 0:W], lhs, rhs, i == 0, i == last)
        if i == last:
            mm.then_inc(S.pm, 1)

    g.sync.wait_ge(S.vy, 1)
    g.sync.dma_start(T.y[:], T.ysb[:]).then_inc(S.sy, 16)
    g.sync.wait_ge(S.sy, 16)
